import numpy as np
import ml_dtypes


def mxq(x, axis, fmt="e4m3"):
    dtype, down = {"e4m3": (ml_dtypes.float8_e4m3fn, 7), "e5m2": (ml_dtypes.float8_e5m2, 14)}[fmt]
    v = np.moveaxis(np.asarray(x, np.float32).astype(ml_dtypes.bfloat16).astype(np.float64), axis, -1)
    blocks = v.reshape(v.shape[:-1] + (-1, 32))
    amax = np.abs(blocks).max(-1, keepdims=True)
    byte = np.maximum(np.where(amax > 0, np.frexp(amax)[1] - 1 + 127, 0) - down, 1)
    scale = np.exp2(byte - 127.0)
    codes = (blocks / scale).astype(np.float32).astype(dtype).astype(np.float64)
    return np.moveaxis((codes * scale).reshape(v.shape), -1, axis)


WIDE = False


def mx_kscale(k):
    if not WIDE:
        return np.ones(k)
    levels = np.array([10, -10, 5, -5, 0])
    if k % 512:
        return np.exp2(np.random.permutation(np.resize(levels, k // 32))).repeat(32)
    a = np.empty((k // 512, 16))
    for p in range(k // 512):
        a[p, :8] = np.random.permutation(np.resize(levels, 8))
        for g in range(8):
            far = levels[np.abs(levels - a[p, g]) >= 10]
            a[p, g + 8] = far[np.random.randint(len(far))]
    return np.exp2(a.ravel()).repeat(32)


BF16 = ml_dtypes.bfloat16


def bf(x):
    return np.asarray(x, np.float32).astype(BF16)


def f64(x):
    return np.asarray(x).astype(np.float64)


E2M1 = np.array([0.0, 0.5, 1.0, 1.5, 2.0, 3.0, 4.0, 6.0, -0.0, -0.5, -1.0, -1.5, -2.0, -3.0, -4.0, -6.0])


def pack_weight(w, fmt):
    k, n = w.shape
    w = f64(bf(w)).reshape(k // 32, 32, n)
    amax = np.abs(w).max(1)
    if fmt == "e4m3":
        byte = np.frexp(amax)[1] - 1 + 127 - 7
    else:
        mant, ex = np.frexp(amax / 6.0)
        byte = np.where(mant > 0.5, ex, ex - 1) + 127
    byte = np.clip(np.where(amax > 0, byte, 1), 1, 254)
    scaled = (w * np.exp2(127.0 - byte)[:, None, :]).reshape(k, n).astype(np.float32)
    by_word = np.ascontiguousarray(scaled.reshape(k // 512, 128, 4, n).transpose(0, 1, 3, 2))
    if fmt == "e4m3":
        words = by_word.astype(ml_dtypes.float8_e4m3fn).view(np.uint8)
    else:
        c = by_word.astype(ml_dtypes.float4_e2m1fn).view(np.uint8) & 0xF
        words = c[..., 0::2] | (c[..., 1::2] << 4)
    return np.ascontiguousarray(words), np.ascontiguousarray(byte.astype(np.uint8).reshape(k // 512, 16, n))


def unpack_weight(words, scales, fmt):
    g, p, n, _ = words.shape
    if fmt == "e4m3":
        vals = np.ascontiguousarray(words).view(ml_dtypes.float8_e4m3fn).astype(np.float64)
    else:
        nib = np.empty((g, p, n, 4), np.uint8)
        nib[..., 0::2] = words & 0xF
        nib[..., 1::2] = words >> 4
        vals = E2M1[nib]
    vals = vals * np.repeat(np.exp2(scales.astype(np.float64) - 127.0), 8, axis=1)[..., None]
    return vals.transpose(0, 1, 3, 2).reshape(g * 512, n)
def pack4(w):
    words, scales = pack_weight(w, "e2m1")
    return words.reshape(words.shape[0], 128, -1), scales


def unpack4(words, scales):
    return unpack_weight(words.reshape(words.shape[0], 128, -1, 2), scales, "e2m1")


P, R, T = 1024, 1024, 2048


def setup_inputs():
    r, s, t = mx_kscale(R), mx_kscale(T), mx_kscale(P)
    gain = np.random.uniform(0.8, 1.25, P)
    lam = np.random.uniform(0.5, 1.5, R)
    f = np.random.standard_normal((R, P)) / np.sqrt(R) * gain
    a_words, a_scales = pack4(f * lam[:, None] * r[:, None])
    b_words, b_scales = pack4(f / r[:, None] * t)
    z = 1.5 * np.random.standard_normal((T, P)) / np.sqrt(T)
    wt = np.random.uniform(0.5, 1.5, T)
    return {"a_words": a_words, "a_scales": a_scales,
            "b_words": b_words, "b_scales": b_scales,
            "xw": bf(z * wt[:, None] * s[:, None] / t),
            "x": bf(z / s[:, None]),
            "d": bf((f * f * lam[:, None]).sum(axis=0))}


def reference(a_words, a_scales, b_words, b_scales, xw, x, d):
    a = unpack4(a_words, a_scales)
    b = unpack4(b_words, b_scales)
    omega = a.T @ b
    cov = mxq(f64(xw), 0, "e4m3").T @ mxq(f64(x), 0, "e4m3")
    y = mxq(omega, 1, "e4m3") @ mxq(cov, 0, "e4m3")
    return y + y.T - np.diag(1.0 / f64(d))

@@ -1,0 +1,435 @@
+from contextlib import ExitStack
+
+import concourse.mybir as mybir
+from concourse.masks import make_identity
+
+FLOPS = 2 * 1024 * 1024 * (1024 + 2048 + 1024)
+
+F32 = mybir.dt.float32
+BF16 = mybir.dt.bfloat16
+I32 = mybir.dt.int32
+U32 = mybir.dt.uint32
+U8 = mybir.dt.uint8
+FP8X4 = mybir.dt.float8_e4m3fn_x4
+FP4X4 = mybir.dt.float4_e2m1fn_x4
+ALU = mybir.AluOpType
+
+P = 128
+
+
+def tile_concord_precision_gradient_s12_kernel(tc, a_words, a_scales, b_words, b_scales, xw, x, d, out):
+    nc = tc.nc
+    with ExitStack() as ctx:
+        keep = ctx.enter_context(tc.tile_pool(name="keep", bufs=1))
+        work = ctx.enter_context(tc.tile_pool(name="work", bufs=5))
+        psum = ctx.enter_context(tc.psum_pool(name="psum", bufs=8))
+        ctx.enter_context(tc.manual_schedule())
+
+        def kt(name, shape, dt):
+            t = keep.tile(shape, dt, name=name, tag=name, align_bytes=64)
+            return t
+
+        def bank():
+            t = psum.tile([P, 512], F32, name="bank", tag="bank")
+            return t
+
+        def copy(eng, dst, src):
+            if eng == "S":
+                nc.scalar.copy(out=dst, in_=src)
+            else:
+                nc.vector.tensor_copy(out=dst, in_=src)
+
+        a_codes = kt("a_codes", [P, 2, 2048], U8)
+        a_sc = kt("a_sc", [P, 2, 1024], U8)
+        b_raw = [kt("b_raw%d" % h, [P, 2, 1024], U8) for h in range(2)]
+        b_codes = kt("b_codes", [P, 2, 2, 1024], U8)
+        b_scr = kt("b_scr", [P, 2, 1024], U8)
+        b_sc = kt("b_sc", [P, 2, 1024], U8)
+        w_raw = [kt("w_raw%d" % c, [P, 4, 1024], BF16) for c in range(4)]
+        x_raw = [kt("x_raw%d" % c, [P, 4, 1024], BF16) for c in range(4)]
+        w_codes = {(h, c): kt("w_codes%d%d" % (h, c), [P, 512], U32) for h in range(2) for c in range(4)}
+        w_sc = {(h, c): kt("w_sc%d%d" % (h, c), [P, 512], U8) for h in range(2) for c in range(4)}
+        x_codes = {(h, c): kt("x_codes%d%d" % (h, c), [P, 512], U32) for h in range(2) for c in range(4)}
+        x_sc = {(h, c): kt("x_sc%d%d" % (h, c), [P, 512], U8) for h in range(2) for c in range(4)}
+        o_codes = kt("o_codes", [P, 2, 1024], U32)
+        o_sc = kt("o_sc", [P, 2, 1024], U8)
+        c_codes = kt("c_codes", [P, 2, 1024], U32)
+        c_sc = kt("c_sc", [P, 2, 1024], U8)
+        og = {(h, q): kt("og%d%d" % (h, q), [P, 512, 4], BF16) for h in range(2) for q in range(2)}
+        kun = {(h, l): kt("kun%d%d" % (h, 0), [P, 4, 512], BF16) for h in range(2) for l in range(1)}
+        for h in range(2):
+            kun[h, 1] = kt("kun%d1" % h, [P, 4, 512], BF16)
+        gs = [kt("gs%d" % b, [P, 128 * (b + 1)], F32) for b in range(8)]
+        ut = {(b, k): kt("ut%d%d" % (b, k), [P, min(4, b - 4 * k), 128], F32) for b in range(8) for k in range((b + 3) // 4)}
+        identx = kt("identx", [P, 512], F32)
+        ident = identx[:, 384:512]
+        d_row = kt("d_row", [P, 128], BF16)
+        d_f32 = kt("d_f32", [P, 128], F32)
+        d_rec = kt("d_rec", [P, 8], F32)
+        d_neg = kt("d_neg", [P, 8], F32)
+        grp = {}
+        ps = {}
+
+        nc.vector.memset(b_scr[:].bitcast(I32), 0)
+        nc.vector.memset(a_sc[:].bitcast(I32), 0)
+        nc.gpsimd.memset(d_row[:], 0.0)
+        nc.gpsimd.dma_start(out=d_row[0:8, :], in_=d.rearrange("(a p) -> a p", p=128))
+        nc.gpsimd.memset(identx[:], 0.0)
+        make_identity(nc, ident)
+        nc.gpsimd.tensor_copy(out=d_f32[:], in_=d_row[:])
+
+        def load_b(h):
+            nc.sync.dma_start(out=b_raw[h][:].bitcast(I32), in_=b_words[:, :, h * 1024 : (h + 1) * 1024].bitcast(I32).rearrange("g p n -> p g n"))
+
+        def load_a(q):
+            nc.sync.dma_start(out=a_codes[:, :, q * 1024 : (q + 1) * 1024].bitcast(I32), in_=a_words[:, :, q * 1024 : (q + 1) * 1024].bitcast(I32).rearrange("g p n -> p g n"))
+
+        def load_sc(eng, dst, src):
+            for q in range(4):
+                eng.dma_start(out=dst[32 * q : 32 * q + 4, :, :].bitcast(I32), in_=src[:, 4 * q : 4 * q + 4, :].bitcast(I32).rearrange("g q n -> q g n"))
+
+        def load_k(dst, src, c, lo, hi):
+            nc.sync.dma_start(out=dst[c][:, :, lo:hi], in_=src[c * 512 : (c + 1) * 512, lo:hi].rearrange("(p j) w -> p j w", j=4))
+
+        load_b(0)
+        load_a(0)
+        load_sc(nc.scalar, b_scr, b_scales)
+        load_sc(nc.scalar, a_sc, a_scales)
+        load_b(1)
+        load_k(w_raw, xw, 0, 0, 512)
+        load_k(w_raw, xw, 0, 512, 1024)
+        load_k(x_raw, x, 0, 0, 512)
+        load_a(1)
+        for c in range(1, 4):
+            load_k(w_raw, xw, c, 0, 1024)
+            load_k(x_raw, x, c, 0, 512)
+        for c in range(4):
+            load_k(x_raw, x, c, 512, 1024)
+
+
+        def pB(h):
+            nc.vector.tensor_copy(
+                out=b_codes[:, :, h, :].bitcast(I32).rearrange("p g (u s w) -> p g u s w", u=4, w=2),
+                in_=b_raw[h][:].bitcast(I32).rearrange("p g (s u w) -> p g u s w", u=4, w=2),
+            )
+            if h == 0:
+                nc.vector.tensor_copy(
+                    out=b_sc[:].bitcast(I32).rearrange("p g (h u s) -> p g h u s", h=2, u=4),
+                    in_=b_scr[:].bitcast(I32).rearrange("p g (h s u) -> p g h u s", h=2, u=4),
+                )
+
+        def Om(h, ib):
+            t = bank()
+            ps["O", h, ib] = t
+            for u in range(4):
+                for g in range(2):
+                    nc.tensor.matmul_mx(
+                        out=t[:, u * 128 : (u + 1) * 128],
+                        lhsT=b_codes[:, g, h, u * 256 : (u + 1) * 256].bitcast(FP4X4),
+                        lhsT_scale=b_sc[:, g, h * 512 + u * 128 : h * 512 + (u + 1) * 128],
+                        rhs=a_codes[:, g, ib * 256 : (ib + 1) * 256].bitcast(FP4X4),
+                        rhs_scale=a_sc[:, g, ib * 128 : (ib + 1) * 128],
+                        start=(g == 0),
+                        stop=(g == 1),
+                    )
+
+        def eO(h, ib, E):
+            n0 = (ib % 4) * 128
+            copy(E, og[h, ib // 4][:, n0 : n0 + 128, :], ps["O", h, ib][:].rearrange("p (u n) -> p n u", u=4))
+
+        def qO(h, q):
+            nc.vector.quantize_mx(out=o_codes[:, h, q * 512 : (q + 1) * 512].bitcast(FP8X4), scales=o_sc[:, h, q * 512 : (q + 1) * 512], in_=og[h, q][:].rearrange("p n t -> p (n t)"))
+
+        def i(k, h, c, E):
+            t = work.tile([P, 2048], BF16, name="grp", tag="grp", align_bytes=64)
+            grp[k, h, c] = t
+            if k == "W":
+                copy(E, t[:].rearrange("p (u s w j) -> p u s j w", u=4, s=32, w=4), w_raw[c][:, :, h * 512 : (h + 1) * 512].rearrange("p j (s u w) -> p u s j w", u=4, w=4))
+            else:
+                copy(E, t[:].rearrange("p (a w j) -> p a j w", w=4, j=4), x_raw[c][:, :, h * 512 : (h + 1) * 512].rearrange("p j (a w) -> p a j w", w=4))
+
+        def q(k, h, c):
+            co, sc = (w_codes, w_sc) if k == "W" else (x_codes, x_sc)
+            nc.vector.quantize_mx(out=co[h, c][:].bitcast(FP8X4), scales=sc[h, c][:], in_=grp[k, h, c][:])
+
+        def K(h, l, u, c):
+            if c == 0:
+                ps["K", h, l, u] = bank()
+            nc.tensor.matmul_mx(
+                out=ps["K", h, l, u][:],
+                lhsT=w_codes[h, c][:, u * 128 : (u + 1) * 128].bitcast(FP8X4),
+                lhsT_scale=w_sc[h, c][:, u * 128 : (u + 1) * 128],
+                rhs=x_codes[l, c][:].bitcast(FP8X4),
+                rhs_scale=x_sc[l, c][:],
+                start=(c == 0),
+                stop=(c == 3),
+            )
+
+        def eK(h, l, u, E):
+            copy(E, kun[h, l][:, u, :], ps["K", h, l, u][:])
+
+        def iK(h, l, E):
+            t = work.tile([P, 2048], BF16, name="grp", tag="grp", align_bytes=64)
+            grp["K", h, l] = t
+            copy(E, t[:].rearrange("p (a w u) -> p a u w", w=4, u=4), kun[h, l][:].rearrange("p u (a w) -> p a u w", w=4))
+
+        def qK(h, l):
+            nc.vector.quantize_mx(out=c_codes[:, h, l * 512 : (l + 1) * 512].bitcast(FP8X4), scales=c_sc[:, h, l * 512 : (l + 1) * 512], in_=grp["K", h, l][:])
+
+        def G(b, k):
+            t = bank()
+            ps["G", b, k] = t
+            lo = 512 * k
+            n = min(512, 128 * (b + 1) - lo)
+            bs = slice(b * 128, (b + 1) * 128)
+            for o, w in ([(0, 256), (256, 128)] if n == 384 else [(0, n)]):
+                ns = slice(lo + o, lo + o + w)
+                step = 0
+                for h in range(2):
+                    for lc, ls, rc, rs in ((o_codes, o_sc, c_codes, c_sc), (c_codes, c_sc, o_codes, o_sc)):
+                        nc.tensor.matmul_mx(
+                            out=t[:, o : o + w],
+                            lhsT=lc[:, h, bs].bitcast(FP8X4),
+                            lhsT_scale=ls[:, h, bs],
+                            rhs=rc[:, h, ns].bitcast(FP8X4),
+                            rhs_scale=rs[:, h, ns],
+                            start=(step == 0),
+                            stop=(step == 3),
+                        )
+                        step += 1
+
+        def eG(b, k, E):
+            lo = 512 * k
+            n = min(512, 128 * (b + 1) - lo)
+            t = ps["G", b, k]
+            if lo + n == 128 * (b + 1):
+                nc.vector.scalar_tensor_tensor(out=gs[b][:, lo : lo + n], in0=identx[:, 512 - n : 512], scalar=d_neg[:, b : b + 1], in1=t[:, 0:n], op0=ALU.mult, op1=ALU.add)
+            else:
+                copy(E, gs[b][:, lo : lo + n], t[:, 0:n])
+            nc.sync.dma_start(out=out[b * 128 : (b + 1) * 128, lo : lo + n], in_=gs[b][:, lo : lo + n])
+
+        def Tr(b, k):
+            t = bank()
+            ps["T", b, k] = t
+            for m in range(min(4, b - 4 * k)):
+                a = 4 * k + m
+                nc.tensor.transpose(t[:, m * 128 : (m + 1) * 128], gs[b][:, a * 128 : (a + 1) * 128], ident)
+
+        def eT(b, k, E):
+            n = min(4, b - 4 * k)
+            copy(E, ut[b, k][:], ps["T", b, k][:, 0 : n * 128].rearrange("p (a w) -> p a w", a=n))
+            nc.sync.dma_start(out=out[512 * k : 512 * k + 128 * n, b * 128 : (b + 1) * 128].rearrange("(a p) w -> p a w", p=128), in_=ut[b, k][:])
+
+        def dT():
+            t = bank()
+            ps["d"] = t
+            nc.tensor.transpose(t[:, 0:128], d_f32[:], ident)
+
+        def dN():
+            nc.vector.reciprocal(out=d_rec[:], in_=ps["d"][:, 0:8])
+            nc.vector.tensor_scalar(out=d_neg[:], in0=d_rec[:], scalar1=-1.0, scalar2=None, op0=ALU.mult)
+
+        pB(0)
+        Om(0, 0)
+        Om(0, 1)
+        pB(1)
+        eO(0, 0, "S")
+        Om(0, 2)
+        eO(0, 1, "S")
+        Om(0, 3)
+        i("W", 0, 0, "V")
+        eO(0, 2, "S")
+        Om(1, 0)
+        eO(0, 3, "S")
+        Om(1, 1)
+        i("W", 1, 0, "S")
+        Om(1, 2)
+        Om(1, 3)
+        i("X", 0, 0, "V")
+        dT()
+        Om(0, 4)
+        eO(1, 0, "S")
+        q("W", 0, 0)
+        Om(0, 5)
+        eO(1, 1, "S")
+        q("W", 1, 0)
+        Om(0, 6)
+        eO(1, 2, "S")
+        q("X", 0, 0)
+        Om(0, 7)
+        eO(1, 3, "S")
+        dN()
+        Om(1, 4)
+        i("W", 1, 1, "V")
+        eO(0, 4, "S")
+        Om(1, 5)
+        eO(0, 5, "S")
+        Om(1, 6)
+        eO(0, 6, "S")
+        i("X", 0, 1, "V")
+        Om(1, 7)
+        eO(0, 7, "S")
+        K(0, 0, 0, 0)
+        i("W", 0, 1, "S")
+        q("W", 1, 1)
+        K(0, 0, 1, 0)
+        K(0, 0, 2, 0)
+        q("X", 0, 1)
+        K(0, 0, 3, 0)
+        eO(1, 6, "V")
+        K(1, 0, 0, 0)
+        eO(1, 4, "S")
+        q("W", 0, 1)
+        eO(1, 5, "S")
+        K(1, 0, 1, 0)
+        eO(1, 7, "V")
+        i("W", 0, 2, "S")
+        K(1, 0, 2, 0)
+        i("W", 1, 2, "V")
+        K(1, 0, 3, 0)
+        K(0, 0, 0, 1)
+        K(0, 0, 1, 1)
+        K(0, 0, 2, 1)
+        i("X", 0, 2, "V")
+        K(0, 0, 3, 1)
+        K(1, 0, 0, 1)
+        K(1, 0, 1, 1)
+        K(1, 0, 2, 1)
+        i("W", 0, 3, "S")
+        K(1, 0, 3, 1)
+        q("W", 1, 2)
+        q("X", 0, 2)
+        q("W", 0, 2)
+        i("W", 1, 3, "V")
+        K(0, 0, 0, 2)
+        i("X", 0, 3, "S")
+        K(0, 0, 1, 2)
+        K(0, 0, 2, 2)
+        K(0, 0, 3, 2)
+        K(1, 0, 0, 2)
+        i("X", 1, 0, "V")
+        K(1, 0, 1, 2)
+        K(1, 0, 2, 2)
+        K(1, 0, 3, 2)
+        q("W", 1, 3)
+        q("W", 0, 3)
+        i("X", 1, 1, "V")
+        q("X", 0, 3)
+        q("X", 1, 0)
+        K(0, 0, 0, 3)
+        K(0, 0, 1, 3)
+        eK(0, 0, 0, "S")
+        qO(0, 0)
+        K(0, 0, 2, 3)
+        K(0, 0, 3, 3)
+        eK(0, 0, 1, "S")
+        q("X", 1, 1)
+        K(1, 0, 0, 3)
+        K(1, 0, 1, 3)
+        eK(0, 0, 2, "S")
+        K(1, 0, 2, 3)
+        i("X", 1, 2, "V")
+        K(1, 0, 3, 3)
+        eK(0, 0, 3, "S")
+        K(0, 1, 0, 0)
+        K(0, 1, 1, 0)
+        eK(1, 0, 0, "S")
+        K(0, 1, 2, 0)
+        eK(1, 0, 1, "V")
+        K(0, 1, 3, 0)
+        eK(1, 0, 2, "S")
+        K(1, 1, 0, 0)
+        eK(1, 0, 3, "V")
+        K(1, 1, 1, 0)
+        i("X", 1, 3, "S")
+        K(1, 1, 2, 0)
+        q("X", 1, 2)
+        K(1, 1, 3, 0)
+        K(0, 1, 0, 1)
+        iK(1, 0, "V")
+        K(0, 1, 1, 1)
+        K(0, 1, 2, 1)
+        K(0, 1, 3, 1)
+        K(1, 1, 0, 1)
+        K(1, 1, 1, 1)
+        K(1, 1, 2, 1)
+        iK(0, 0, "S")
+        q("X", 1, 3)
+        K(1, 1, 3, 1)
+        K(0, 1, 0, 2)
+        qO(1, 0)
+        K(0, 1, 1, 2)
+        K(0, 1, 2, 2)
+        K(0, 1, 3, 2)
+        qK(1, 0)
+        K(1, 1, 0, 2)
+        K(1, 1, 1, 2)
+        qO(0, 1)
+        K(1, 1, 2, 2)
+        K(1, 1, 3, 2)
+        qO(1, 1)
+        K(0, 1, 0, 3)
+        K(0, 1, 1, 3)
+        eK(0, 1, 0, "S")
+        qK(0, 0)
+        K(0, 1, 2, 3)
+        K(0, 1, 3, 3)
+        eK(0, 1, 1, "S")
+        K(1, 1, 0, 3)
+        K(1, 1, 1, 3)
+        eK(1, 1, 0, "V")
+        eK(0, 1, 2, "S")
+        K(1, 1, 2, 3)
+        K(1, 1, 3, 3)
+        eK(1, 1, 1, "V")
+        eK(0, 1, 3, "S")
+        G(3, 0)
+        eK(1, 1, 2, "V")
+        iK(0, 1, "S")
+        eK(1, 1, 3, "V")
+        G(2, 0)
+        iK(1, 1, "V")
+        G(1, 0)
+        G(0, 0)
+        qK(0, 1)
+        qK(1, 1)
+        eG(3, 0, "V")
+        G(4, 1)
+        G(4, 0)
+        eG(2, 0, "V")
+        eG(1, 0, "V")
+        eG(0, 0, "V")
+        Tr(3, 0)
+        eG(4, 1, "V")
+        eG(4, 0, "S")
+        Tr(2, 0)
+        eT(3, 0, "S")
+        Tr(1, 0)
+        eT(2, 0, "V")
+        G(5, 1)
+        eT(1, 0, "V")
+        G(5, 0)
+        eG(5, 1, "V")
+        Tr(4, 0)
+        eG(5, 0, "S")
+        G(6, 1)
+        eT(4, 0, "S")
+        G(6, 0)
+        eG(6, 1, "V")
+        Tr(5, 1)
+        eG(6, 0, "S")
+        Tr(5, 0)
+        eT(5, 1, "S")
+        G(7, 0)
+        eT(5, 0, "V")
+        Tr(6, 0)
+        eG(7, 0, "S")
+        Tr(6, 1)
+        eT(6, 0, "S")
+        G(7, 1)
+        eT(6, 1, "V")
+        Tr(7, 0)
+        eG(7, 1, "V")
+        eT(7, 0, "S")
+        Tr(7, 1)
+        eT(7, 1, "V")

@@ -39,14 +39,14 @@ def tile_concord_precision_gradient_s12_kernel(tc, a_words, a_scales, b_words, b
             else:
                 nc.vector.tensor_copy(out=dst, in_=src)
 
-        a_codes = kt("a_codes", [P, 2, 2048], U8)
+        a_codes = [kt("a_codes%d" % h, [P, 2, 1024], U8) for h in range(2)]
         a_sc = kt("a_sc", [P, 2, 1024], U8)
         b_raw = [kt("b_raw%d" % h, [P, 2, 1024], U8) for h in range(2)]
-        b_codes = kt("b_codes", [P, 2, 2, 1024], U8)
+        b_codes = [kt("b_codes%d" % h, [P, 2, 1024], U8) for h in range(2)]
         b_scr = kt("b_scr", [P, 2, 1024], U8)
         b_sc = kt("b_sc", [P, 2, 1024], U8)
-        w_raw = [kt("w_raw%d" % c, [P, 4, 1024], BF16) for c in range(4)]
-        x_raw = [kt("x_raw%d" % c, [P, 4, 1024], BF16) for c in range(4)]
+        w_raw = {(h, c): kt("w_raw%d%d" % (h, c), [P, 4, 512], BF16) for c in range(4) for h in range(2)}
+        x_raw = {(h, c): kt("x_raw%d%d" % (h, c), [P, 4, 512], BF16) for c in range(4) for h in range(2)}
         w_codes = {(h, c): kt("w_codes%d%d" % (h, c), [P, 512], U32) for h in range(2) for c in range(4)}
         w_sc = {(h, c): kt("w_sc%d%d" % (h, c), [P, 512], U8) for h in range(2) for c in range(4)}
         x_codes = {(h, c): kt("x_codes%d%d" % (h, c), [P, 512], U32) for h in range(2) for c in range(4)}
@@ -59,9 +59,14 @@ def tile_concord_precision_gradient_s12_kernel(tc, a_words, a_scales, b_words, b
         kun = {(h, l): kt("kun%d%d" % (h, 0), [P, 4, 512], BF16) for h in range(2) for l in range(1)}
         for h in range(2):
             kun[h, 1] = kt("kun%d1" % h, [P, 4, 512], BF16)
-        gs = [kt("gs%d" % b, [P, 128 * (b + 1)], F32) for b in range(8)]
-        ut = {(b, k): kt("ut%d%d" % (b, k), [P, min(4, b - 4 * k), 128], F32) for b in range(8) for k in range((b + 3) // 4)}
-        identx = kt("identx", [P, 512], F32)
+        gs = {(0, b): kt("gs0%d" % b, [P, 512], F32) for b in range(4)}
+        for b in range(4, 8):
+            gs[1, b] = kt("gs1%d" % b, [P, 512], F32)
+            gs[2, b] = kt("gs2%d" % b, [P, 128 * (b - 3)], F32)
+        ut = {(0, a): kt("ut0%d" % a, [P, 512], F32) for a in range(4)}
+        for a in range(4, 7):
+            ut[1, a] = kt("ut1%d" % a, [P, 128 * (7 - a)], F32)
+        identx = kt("identx", [P, 896], F32)
         ident = identx[:, 384:512]
         d_row = kt("d_row", [P, 128], BF16)
         d_f32 = kt("d_f32", [P, 128], F32)
@@ -72,51 +77,59 @@ def tile_concord_precision_gradient_s12_kernel(tc, a_words, a_scales, b_words, b
 
         nc.vector.memset(b_scr[:].bitcast(I32), 0)
         nc.vector.memset(a_sc[:].bitcast(I32), 0)
+
+        def load_b(h):
+            nc.sync.dma_start(out=b_raw[h][:].bitcast(I32), in_=b_words[:, :, h * 1024 : (h + 1) * 1024].bitcast(I32).rearrange("g p n -> p g n"))
+
+        def load_a(q):
+            nc.sync.dma_start(out=a_codes[q][:].bitcast(I32), in_=a_words[:, :, q * 1024 : (q + 1) * 1024].bitcast(I32).rearrange("g p n -> p g n"))
+
+        def load_sc(eng, dst, src):
+            for q in range(4):
+                eng.dma_start(out=dst[32 * q : 32 * q + 4, :, :].bitcast(I32), in_=src[:, 4 * q : 4 * q + 4, :].bitcast(I32).rearrange("g q n -> q g n"))
+
+        def load_k(dst, src, h, c):
+            nc.sync.dma_start(out=dst[h, c][:], in_=src[c * 512 : (c + 1) * 512, h * 512 : (h + 1) * 512].rearrange("(p j) w -> p j w", j=4))
+
+        load_sc(nc.sync, a_sc, a_scales)
+        load_sc(nc.sync, b_scr, b_scales)
+        load_b(0)
+        load_a(1)
+        load_a(0)
+        load_b(1)
+        load_k(x_raw, x, 0, 0)
+        load_k(w_raw, xw, 0, 1)
+        load_k(w_raw, xw, 1, 0)
+        load_k(w_raw, xw, 0, 2)
+        load_k(x_raw, x, 0, 1)
+        load_k(w_raw, xw, 1, 1)
+        load_k(w_raw, xw, 0, 0)
+        load_k(w_raw, xw, 1, 2)
+        load_k(w_raw, xw, 0, 3)
+        load_k(x_raw, x, 0, 2)
+        load_k(x_raw, x, 0, 3)
+        load_k(w_raw, xw, 1, 3)
+        load_k(x_raw, x, 1, 1)
+        load_k(x_raw, x, 1, 3)
+        load_k(x_raw, x, 1, 2)
+        load_k(x_raw, x, 1, 0)
         nc.gpsimd.memset(d_row[:], 0.0)
         nc.gpsimd.dma_start(out=d_row[0:8, :], in_=d.rearrange("(a p) -> a p", p=128))
         nc.gpsimd.memset(identx[:], 0.0)
         make_identity(nc, ident)
         nc.gpsimd.tensor_copy(out=d_f32[:], in_=d_row[:])
 
-        def load_b(h):
-            nc.sync.dma_start(out=b_raw[h][:].bitcast(I32), in_=b_words[:, :, h * 1024 : (h + 1) * 1024].bitcast(I32).rearrange("g p n -> p g n"))
-
-        def load_a(q):
-            nc.sync.dma_start(out=a_codes[:, :, q * 1024 : (q + 1) * 1024].bitcast(I32), in_=a_words[:, :, q * 1024 : (q + 1) * 1024].bitcast(I32).rearrange("g p n -> p g n"))
-
-        def load_sc(eng, dst, src):
-            for q in range(4):
-                eng.dma_start(out=dst[32 * q : 32 * q + 4, :, :].bitcast(I32), in_=src[:, 4 * q : 4 * q + 4, :].bitcast(I32).rearrange("g q n -> q g n"))
-
-        def load_k(dst, src, c, lo, hi):
-            nc.sync.dma_start(out=dst[c][:, :, lo:hi], in_=src[c * 512 : (c + 1) * 512, lo:hi].rearrange("(p j) w -> p j w", j=4))
-
-        load_b(0)
-        load_a(0)
-        load_sc(nc.scalar, b_scr, b_scales)
-        load_sc(nc.scalar, a_sc, a_scales)
-        load_b(1)
-        load_k(w_raw, xw, 0, 0, 512)
-        load_k(w_raw, xw, 0, 512, 1024)
-        load_k(x_raw, x, 0, 0, 512)
-        load_a(1)
-        for c in range(1, 4):
-            load_k(w_raw, xw, c, 0, 1024)
-            load_k(x_raw, x, c, 0, 512)
-        for c in range(4):
-            load_k(x_raw, x, c, 512, 1024)
-
+        def pS():
+            nc.vector.tensor_copy(
+                out=b_sc[:].bitcast(I32).rearrange("p g (h u s) -> p g h u s", h=2, u=4),
+                in_=b_scr[:].bitcast(I32).rearrange("p g (h s u) -> p g h u s", h=2, u=4),
+            )
 
         def pB(h):
             nc.vector.tensor_copy(
-                out=b_codes[:, :, h, :].bitcast(I32).rearrange("p g (u s w) -> p g u s w", u=4, w=2),
+                out=b_codes[h][:].bitcast(I32).rearrange("p g (u s w) -> p g u s w", u=4, w=2),
                 in_=b_raw[h][:].bitcast(I32).rearrange("p g (s u w) -> p g u s w", u=4, w=2),
             )
-            if h == 0:
-                nc.vector.tensor_copy(
-                    out=b_sc[:].bitcast(I32).rearrange("p g (h u s) -> p g h u s", h=2, u=4),
-                    in_=b_scr[:].bitcast(I32).rearrange("p g (h s u) -> p g h u s", h=2, u=4),
-                )
 
         def Om(h, ib):
             t = bank()
@@ -125,9 +138,9 @@ def tile_concord_precision_gradient_s12_kernel(tc, a_words, a_scales, b_words, b
                 for g in range(2):
                     nc.tensor.matmul_mx(
                         out=t[:, u * 128 : (u + 1) * 128],
-                        lhsT=b_codes[:, g, h, u * 256 : (u + 1) * 256].bitcast(FP4X4),
+                        lhsT=b_codes[h][:, g, u * 256 : (u + 1) * 256].bitcast(FP4X4),
                         lhsT_scale=b_sc[:, g, h * 512 + u * 128 : h * 512 + (u + 1) * 128],
-                        rhs=a_codes[:, g, ib * 256 : (ib + 1) * 256].bitcast(FP4X4),
+                        rhs=a_codes[ib // 4][:, g, (ib % 4) * 256 : (ib % 4 + 1) * 256].bitcast(FP4X4),
                         rhs_scale=a_sc[:, g, ib * 128 : (ib + 1) * 128],
                         start=(g == 0),
                         stop=(g == 1),
@@ -144,9 +157,9 @@ def tile_concord_precision_gradient_s12_kernel(tc, a_words, a_scales, b_words, b
             t = work.tile([P, 2048], BF16, name="grp", tag="grp", align_bytes=64)
             grp[k, h, c] = t
             if k == "W":
-                copy(E, t[:].rearrange("p (u s w j) -> p u s j w", u=4, s=32, w=4), w_raw[c][:, :, h * 512 : (h + 1) * 512].rearrange("p j (s u w) -> p u s j w", u=4, w=4))
+                copy(E, t[:].rearrange("p (u s w j) -> p u s j w", u=4, s=32, w=4), w_raw[h, c][:].rearrange("p j (s u w) -> p u s j w", u=4, w=4))
             else:
-                copy(E, t[:].rearrange("p (a w j) -> p a j w", w=4, j=4), x_raw[c][:, :, h * 512 : (h + 1) * 512].rearrange("p j (a w) -> p a j w", w=4))
+                copy(E, t[:].rearrange("p (a w j) -> p a j w", w=4, j=4), x_raw[h, c][:].rearrange("p j (a w) -> p a j w", w=4))
 
         def q(k, h, c):
             co, sc = (w_codes, w_sc) if k == "W" else (x_codes, x_sc)
@@ -176,11 +189,13 @@ def tile_concord_precision_gradient_s12_kernel(tc, a_words, a_scales, b_words, b
         def qK(h, l):
             nc.vector.quantize_mx(out=c_codes[:, h, l * 512 : (l + 1) * 512].bitcast(FP8X4), scales=c_sc[:, h, l * 512 : (l + 1) * 512], in_=grp["K", h, l][:])
 
-        def G(b, k):
+        def span(p, b):
+            return (512, 128 * (b - 3)) if p == 2 else (0, 512)
+
+        def G(p, b):
             t = bank()
-            ps["G", b, k] = t
-            lo = 512 * k
-            n = min(512, 128 * (b + 1) - lo)
+            ps["G", p, b] = t
+            lo, n = span(p, b)
             bs = slice(b * 128, (b + 1) * 128)
             for o, w in ([(0, 256), (256, 128)] if n == 384 else [(0, n)]):
                 ns = slice(lo + o, lo + o + w)
@@ -198,27 +213,29 @@ def tile_concord_precision_gradient_s12_kernel(tc, a_words, a_scales, b_words, b
                         )
                         step += 1
 
-        def eG(b, k, E):
-            lo = 512 * k
-            n = min(512, 128 * (b + 1) - lo)
-            t = ps["G", b, k]
-            if lo + n == 128 * (b + 1):
-                nc.vector.scalar_tensor_tensor(out=gs[b][:, lo : lo + n], in0=identx[:, 512 - n : 512], scalar=d_neg[:, b : b + 1], in1=t[:, 0:n], op0=ALU.mult, op1=ALU.add)
+        def eG(p, b, E):
+            lo, n = span(p, b)
+            t = ps["G", p, b]
+            g = gs[p, b]
+            if p == 1:
+                copy(E, g[:], t[:])
             else:
-                copy(E, gs[b][:, lo : lo + n], t[:, 0:n])
-            nc.sync.dma_start(out=out[b * 128 : (b + 1) * 128, lo : lo + n], in_=gs[b][:, lo : lo + n])
+                z = 384 - (b * 128 - lo)
+                nc.vector.scalar_tensor_tensor(out=g[:], in0=identx[:, z : z + n], scalar=d_neg[:, b : b + 1], in1=t[:, 0:n], op0=ALU.mult, op1=ALU.add)
+            nc.sync.dma_start(out=out[b * 128 : (b + 1) * 128, lo : lo + n], in_=g[:])
 
-        def Tr(b, k):
+        def Tr(p, a):
             t = bank()
-            ps["T", b, k] = t
-            for m in range(min(4, b - 4 * k)):
-                a = 4 * k + m
-                nc.tensor.transpose(t[:, m * 128 : (m + 1) * 128], gs[b][:, a * 128 : (a + 1) * 128], ident)
+            ps["T", p, a] = t
+            for m, b in enumerate(range(4, 8) if p == 0 else range(a + 1, 8)):
+                src = gs[1, b][:, a * 128 : (a + 1) * 128] if p == 0 else gs[2, b][:, a * 128 - 512 : a * 128 - 384]
+                nc.tensor.transpose(t[:, m * 128 : (m + 1) * 128], src, ident)
 
-        def eT(b, k, E):
-            n = min(4, b - 4 * k)
-            copy(E, ut[b, k][:], ps["T", b, k][:, 0 : n * 128].rearrange("p (a w) -> p a w", a=n))
-            nc.sync.dma_start(out=out[512 * k : 512 * k + 128 * n, b * 128 : (b + 1) * 128].rearrange("(a p) w -> p a w", p=128), in_=ut[b, k][:])
+        def eT(p, a, E):
+            u = ut[p, a]
+            n = 512 if p == 0 else 128 * (7 - a)
+            copy(E, u[:], ps["T", p, a][:, 0:n])
+            nc.sync.dma_start(out=out[a * 128 : (a + 1) * 128, 1024 - n : 1024], in_=u[:])
 
         def dT():
             t = bank()
@@ -229,207 +246,202 @@ def tile_concord_precision_gradient_s12_kernel(tc, a_words, a_scales, b_words, b
             nc.vector.reciprocal(out=d_rec[:], in_=ps["d"][:, 0:8])
             nc.vector.tensor_scalar(out=d_neg[:], in0=d_rec[:], scalar1=-1.0, scalar2=None, op0=ALU.mult)
 
+        dT()
+        pS()
         pB(0)
-        Om(0, 0)
-        Om(0, 1)
-        pB(1)
-        eO(0, 0, "S")
-        Om(0, 2)
-        eO(0, 1, "S")
+        dN()
+        Om(0, 4)
         Om(0, 3)
-        i("W", 0, 0, "V")
-        eO(0, 2, "S")
-        Om(1, 0)
+        eO(0, 4, "V")
+        Om(0, 0)
+        pB(1)
         eO(0, 3, "S")
         Om(1, 1)
-        i("W", 1, 0, "S")
-        Om(1, 2)
-        Om(1, 3)
+        eO(0, 0, "S")
         i("X", 0, 0, "V")
-        dT()
-        Om(0, 4)
-        eO(1, 0, "S")
-        q("W", 0, 0)
-        Om(0, 5)
-        eO(1, 1, "S")
-        q("W", 1, 0)
-        Om(0, 6)
-        eO(1, 2, "S")
-        q("X", 0, 0)
-        Om(0, 7)
-        eO(1, 3, "S")
-        dN()
-        Om(1, 4)
-        i("W", 1, 1, "V")
-        eO(0, 4, "S")
-        Om(1, 5)
-        eO(0, 5, "S")
-        Om(1, 6)
-        eO(0, 6, "S")
-        i("X", 0, 1, "V")
         Om(1, 7)
-        eO(0, 7, "S")
-        K(0, 0, 0, 0)
+        eO(1, 1, "S")
+        Om(1, 4)
         i("W", 0, 1, "S")
-        q("W", 1, 1)
-        K(0, 0, 1, 0)
-        K(0, 0, 2, 0)
-        q("X", 0, 1)
-        K(0, 0, 3, 0)
-        eO(1, 6, "V")
-        K(1, 0, 0, 0)
-        eO(1, 4, "S")
-        q("W", 0, 1)
-        eO(1, 5, "S")
-        K(1, 0, 1, 0)
         eO(1, 7, "V")
-        i("W", 0, 2, "S")
-        K(1, 0, 2, 0)
-        i("W", 1, 2, "V")
+        Om(0, 7)
+        q("X", 0, 0)
+        Om(0, 2)
+        i("W", 1, 0, "V")
+        Om(0, 1)
+        Om(1, 6)
+        eO(0, 2, "S")
+        q("W", 0, 1)
+        Om(1, 3)
+        eO(1, 6, "S")
+        q("W", 1, 0)
+        Om(0, 5)
+        eO(1, 4, "S")
+        i("W", 0, 2, "V")
+        Om(1, 0)
+        i("X", 0, 1, "S")
+        K(1, 0, 0, 0)
+        Om(1, 5)
+        eO(0, 1, "V")
         K(1, 0, 3, 0)
-        K(0, 0, 0, 1)
-        K(0, 0, 1, 1)
-        K(0, 0, 2, 1)
-        i("X", 0, 2, "V")
-        K(0, 0, 3, 1)
-        K(1, 0, 0, 1)
-        K(1, 0, 1, 1)
-        K(1, 0, 2, 1)
-        i("W", 0, 3, "S")
-        K(1, 0, 3, 1)
-        q("W", 1, 2)
-        q("X", 0, 2)
+        i("W", 1, 1, "V")
+        K(1, 0, 2, 0)
+        eO(0, 5, "S")
         q("W", 0, 2)
+        i("W", 0, 0, "S")
+        q("X", 0, 1)
+        q("W", 1, 1)
+        i("W", 1, 2, "V")
+        K(1, 0, 2, 1)
+        K(1, 0, 1, 0)
+        eO(0, 7, "S")
+        K(1, 0, 0, 1)
+        K(1, 0, 3, 1)
+        q("W", 0, 0)
+        K(1, 0, 1, 1)
+        i("X", 0, 2, "S")
+        Om(1, 2)
+        i("W", 0, 3, "V")
+        q("W", 1, 2)
+        eO(1, 0, "S")
+        q("X", 0, 2)
+        eO(1, 5, "S")
+        K(0, 0, 1, 0)
         i("W", 1, 3, "V")
-        K(0, 0, 0, 2)
-        i("X", 0, 3, "S")
-        K(0, 0, 1, 2)
-        K(0, 0, 2, 2)
-        K(0, 0, 3, 2)
-        K(1, 0, 0, 2)
-        i("X", 1, 0, "V")
-        K(1, 0, 1, 2)
         K(1, 0, 2, 2)
+        eO(1, 3, "S")
+        K(0, 0, 1, 1)
         K(1, 0, 3, 2)
+        eO(1, 2, "S")
+        K(0, 0, 0, 0)
+        i("X", 0, 3, "V")
+        K(0, 0, 3, 0)
+        i("X", 1, 1, "S")
+        K(0, 0, 3, 1)
+        K(0, 0, 2, 0)
+        K(1, 0, 1, 2)
+        K(1, 0, 0, 2)
         q("W", 1, 3)
-        q("W", 0, 3)
-        i("X", 1, 1, "V")
+        K(0, 0, 2, 1)
+        K(0, 0, 1, 2)
         q("X", 0, 3)
-        q("X", 1, 0)
-        K(0, 0, 0, 3)
-        K(0, 0, 1, 3)
-        eK(0, 0, 0, "S")
-        qO(0, 0)
-        K(0, 0, 2, 3)
-        K(0, 0, 3, 3)
-        eK(0, 0, 1, "S")
-        q("X", 1, 1)
-        K(1, 0, 0, 3)
-        K(1, 0, 1, 3)
-        eK(0, 0, 2, "S")
-        K(1, 0, 2, 3)
-        i("X", 1, 2, "V")
+        K(0, 0, 0, 1)
+        K(0, 0, 0, 2)
+        q("W", 0, 3)
+        K(0, 0, 3, 2)
+        i("X", 1, 2, "S")
         K(1, 0, 3, 3)
+        i("X", 1, 0, "V")
+        K(1, 0, 2, 3)
+        K(0, 0, 3, 3)
+        K(0, 0, 2, 2)
+        K(1, 0, 1, 3)
+        K(1, 0, 0, 3)
+        eK(1, 0, 3, "V")
+        K(0, 0, 1, 3)
+        K(0, 0, 0, 3)
+        q("X", 1, 0)
+        eK(1, 0, 2, "S")
+        K(0, 0, 2, 3)
+        Om(0, 6)
+        q("X", 1, 1)
+        eK(1, 0, 1, "S")
+        K(1, 1, 3, 0)
         eK(0, 0, 3, "S")
+        eO(0, 6, "V")
+        K(0, 1, 3, 0)
+        K(1, 1, 3, 1)
+        eK(0, 0, 2, "S")
+        q("X", 1, 2)
+        K(0, 1, 3, 1)
+        K(1, 1, 1, 0)
+        eK(1, 0, 0, "S")
+        qO(1, 1)
         K(0, 1, 0, 0)
         K(0, 1, 1, 0)
-        eK(1, 0, 0, "S")
-        K(0, 1, 2, 0)
-        eK(1, 0, 1, "V")
-        K(0, 1, 3, 0)
-        eK(1, 0, 2, "S")
-        K(1, 1, 0, 0)
-        eK(1, 0, 3, "V")
-        K(1, 1, 1, 0)
-        i("X", 1, 3, "S")
-        K(1, 1, 2, 0)
-        q("X", 1, 2)
-        K(1, 1, 3, 0)
-        K(0, 1, 0, 1)
-        iK(1, 0, "V")
+        eK(0, 0, 0, "S")
+        i("X", 1, 3, "V")
         K(0, 1, 1, 1)
-        K(0, 1, 2, 1)
-        K(0, 1, 3, 1)
-        K(1, 1, 0, 1)
+        K(1, 1, 2, 0)
+        eK(0, 0, 1, "S")
         K(1, 1, 1, 1)
-        K(1, 1, 2, 1)
+        K(0, 1, 2, 0)
         iK(0, 0, "S")
-        q("X", 1, 3)
-        K(1, 1, 3, 1)
-        K(0, 1, 0, 2)
-        qO(1, 0)
-        K(0, 1, 1, 2)
-        K(0, 1, 2, 2)
         K(0, 1, 3, 2)
+        K(1, 1, 0, 0)
+        q("X", 1, 3)
+        K(0, 1, 2, 1)
+        K(0, 1, 2, 2)
+        qO(0, 0)
+        K(0, 1, 1, 2)
+        K(1, 1, 3, 2)
+        iK(1, 0, "V")
+        K(0, 1, 0, 1)
+        K(0, 1, 3, 3)
+        K(1, 1, 2, 1)
+        eK(0, 1, 3, "S")
+        K(1, 1, 2, 2)
+        K(1, 1, 3, 3)
+        qO(1, 0)
+        K(0, 1, 1, 3)
+        eK(1, 1, 3, "S")
+        K(1, 1, 2, 3)
         qK(1, 0)
+        K(1, 1, 0, 1)
+        eK(1, 1, 2, "S")
         K(1, 1, 0, 2)
+        qK(0, 0)
+        K(0, 1, 0, 2)
+        eK(0, 1, 1, "S")
+        K(0, 1, 0, 3)
+        K(0, 1, 2, 3)
+        eK(0, 1, 0, "V")
+        K(1, 1, 0, 3)
+        eK(0, 1, 2, "S")
         K(1, 1, 1, 2)
         qO(0, 1)
-        K(1, 1, 2, 2)
-        K(1, 1, 3, 2)
-        qO(1, 1)
-        K(0, 1, 0, 3)
-        K(0, 1, 1, 3)
-        eK(0, 1, 0, "S")
-        qK(0, 0)
-        K(0, 1, 2, 3)
-        K(0, 1, 3, 3)
-        eK(0, 1, 1, "S")
-        K(1, 1, 0, 3)
         K(1, 1, 1, 3)
-        eK(1, 1, 0, "V")
-        eK(0, 1, 2, "S")
-        K(1, 1, 2, 3)
-        K(1, 1, 3, 3)
-        eK(1, 1, 1, "V")
-        eK(0, 1, 3, "S")
-        G(3, 0)
-        eK(1, 1, 2, "V")
-        iK(0, 1, "S")
-        eK(1, 1, 3, "V")
-        G(2, 0)
-        iK(1, 1, "V")
-        G(1, 0)
         G(0, 0)
-        qK(0, 1)
+        eK(1, 1, 1, "S")
+        eK(1, 1, 0, "V")
+        iK(0, 1, "S")
+        iK(1, 1, "V")
+        G(0, 1)
+        G(0, 2)
         qK(1, 1)
-        eG(3, 0, "V")
-        G(4, 1)
-        G(4, 0)
-        eG(2, 0, "V")
-        eG(1, 0, "V")
+        qK(0, 1)
+        G(0, 3)
+        G(1, 4)
+        eG(0, 3, "V")
+        eG(0, 1, "V")
+        G(1, 7)
+        eG(1, 4, "V")
         eG(0, 0, "V")
-        Tr(3, 0)
-        eG(4, 1, "V")
-        eG(4, 0, "S")
-        Tr(2, 0)
-        eT(3, 0, "S")
-        Tr(1, 0)
-        eT(2, 0, "V")
-        G(5, 1)
-        eT(1, 0, "V")
-        G(5, 0)
-        eG(5, 1, "V")
-        Tr(4, 0)
-        eG(5, 0, "S")
-        G(6, 1)
-        eT(4, 0, "S")
-        G(6, 0)
-        eG(6, 1, "V")
-        Tr(5, 1)
-        eG(6, 0, "S")
-        Tr(5, 0)
-        eT(5, 1, "S")
-        G(7, 0)
-        eT(5, 0, "V")
-        Tr(6, 0)
-        eG(7, 0, "S")
-        Tr(6, 1)
-        eT(6, 0, "S")
-        G(7, 1)
-        eT(6, 1, "V")
-        Tr(7, 0)
-        eG(7, 1, "V")
-        eT(7, 0, "S")
-        Tr(7, 1)
-        eT(7, 1, "V")
+        G(1, 5)
+        eG(1, 7, "S")
+        eG(0, 2, "V")
+        G(1, 6)
+        eG(1, 5, "V")
+        G(2, 7)
+        eG(1, 6, "S")
+        Tr(0, 0)
+        eG(2, 7, "V")
+        Tr(0, 3)
+        eT(0, 0, "S")
+        Tr(0, 2)
+        eT(0, 3, "V")
+        G(2, 6)
+        eT(0, 2, "S")
+        Tr(0, 1)
+        eG(2, 6, "V")
+        G(2, 5)
+        eT(0, 1, "S")
+        Tr(1, 5)
+        eG(2, 5, "V")
+        Tr(1, 6)
+        eT(1, 5, "V")
+        G(2, 4)
+        Tr(1, 4)
+        eG(2, 4, "V")
+        eT(1, 6, "V")
+        eT(1, 4, "S")

@@ -45,7 +45,8 @@ def tile_concord_precision_gradient_s12_kernel(tc, a_words, a_scales, b_words, b
         b_codes = [kt("b_codes%d" % h, [P, 2, 1024], U8) for h in range(2)]
         b_scr = kt("b_scr", [P, 2, 1024], U8)
         b_sc = kt("b_sc", [P, 2, 1024], U8)
-        w_raw = {(h, c): kt("w_raw%d%d" % (h, c), [P, 4, 512], BF16) for c in range(4) for h in range(2)}
+        w_rawf = {c: kt("w_raw%d" % c, [P, 4, 1024], BF16) for c in range(1, 4)}
+        w_raw = {(h, 0): kt("w_raw0%d" % h, [P, 4, 512], BF16) for h in range(2)}
         x_raw = {(h, c): kt("x_raw%d%d" % (h, c), [P, 4, 512], BF16) for c in range(4) for h in range(2)}
         w_codes = {(h, c): kt("w_codes%d%d" % (h, c), [P, 512], U32) for h in range(2) for c in range(4)}
         w_sc = {(h, c): kt("w_sc%d%d" % (h, c), [P, 512], U8) for h in range(2) for c in range(4)}
@@ -56,17 +57,17 @@ def tile_concord_precision_gradient_s12_kernel(tc, a_words, a_scales, b_words, b
         c_codes = kt("c_codes", [P, 2, 1024], U32)
         c_sc = kt("c_sc", [P, 2, 1024], U8)
         og = {(h, q): kt("og%d%d" % (h, q), [P, 512, 4], BF16) for h in range(2) for q in range(2)}
-        kun = {(h, l): kt("kun%d%d" % (h, 0), [P, 4, 512], BF16) for h in range(2) for l in range(1)}
-        for h in range(2):
-            kun[h, 1] = kt("kun%d1" % h, [P, 4, 512], BF16)
-        gs = {(0, b): kt("gs0%d" % b, [P, 512], F32) for b in range(4)}
+        kg = {(h, l): kt("kg%d%d" % (h, l), [P, 512, 4], BF16) for h in range(2) for l in range(2)}
+        gs = {(0, b): kt("gs0%d" % b, [P, 128 * (b + 1)], F32) for b in range(4)}
         for b in range(4, 8):
             gs[1, b] = kt("gs1%d" % b, [P, 512], F32)
             gs[2, b] = kt("gs2%d" % b, [P, 128 * (b - 3)], F32)
         ut = {(0, a): kt("ut0%d" % a, [P, 512], F32) for a in range(4)}
+        for a in range(3):
+            ut[2, a] = kt("ut2%d" % a, [P, 128 * (3 - a)], F32)
         for a in range(4, 7):
             ut[1, a] = kt("ut1%d" % a, [P, 128 * (7 - a)], F32)
-        identx = kt("identx", [P, 896], F32)
+        identx = kt("identx", [P, 512], F32)
         ident = identx[:, 384:512]
         d_row = kt("d_row", [P, 128], BF16)
         d_f32 = kt("d_f32", [P, 128], F32)
@@ -88,31 +89,31 @@ def tile_concord_precision_gradient_s12_kernel(tc, a_words, a_scales, b_words, b
             for q in range(4):
                 eng.dma_start(out=dst[32 * q : 32 * q + 4, :, :].bitcast(I32), in_=src[:, 4 * q : 4 * q + 4, :].bitcast(I32).rearrange("g q n -> q g n"))
 
+        def load_w(c):
+            nc.sync.dma_start(out=w_rawf[c][:], in_=xw[c * 512 : (c + 1) * 512, :].rearrange("(p j) w -> p j w", j=4))
+
         def load_k(dst, src, h, c):
             nc.sync.dma_start(out=dst[h, c][:], in_=src[c * 512 : (c + 1) * 512, h * 512 : (h + 1) * 512].rearrange("(p j) w -> p j w", j=4))
 
+        load_a(0)
         load_sc(nc.sync, a_sc, a_scales)
         load_sc(nc.sync, b_scr, b_scales)
         load_b(0)
-        load_a(1)
-        load_a(0)
-        load_b(1)
         load_k(x_raw, x, 0, 0)
-        load_k(w_raw, xw, 0, 1)
-        load_k(w_raw, xw, 1, 0)
-        load_k(w_raw, xw, 0, 2)
-        load_k(x_raw, x, 0, 1)
-        load_k(w_raw, xw, 1, 1)
+        load_w(2)
+        load_b(1)
+        load_w(1)
+        load_a(1)
         load_k(w_raw, xw, 0, 0)
-        load_k(w_raw, xw, 1, 2)
-        load_k(w_raw, xw, 0, 3)
-        load_k(x_raw, x, 0, 2)
+        load_k(w_raw, xw, 1, 0)
+        load_k(x_raw, x, 0, 1)
         load_k(x_raw, x, 0, 3)
-        load_k(w_raw, xw, 1, 3)
+        load_k(x_raw, x, 0, 2)
+        load_w(3)
+        load_k(x_raw, x, 1, 0)
+        load_k(x_raw, x, 1, 2)
         load_k(x_raw, x, 1, 1)
         load_k(x_raw, x, 1, 3)
-        load_k(x_raw, x, 1, 2)
-        load_k(x_raw, x, 1, 0)
         nc.gpsimd.memset(d_row[:], 0.0)
         nc.gpsimd.dma_start(out=d_row[0:8, :], in_=d.rearrange("(a p) -> a p", p=128))
         nc.gpsimd.memset(identx[:], 0.0)
@@ -157,7 +158,7 @@ def tile_concord_precision_gradient_s12_kernel(tc, a_words, a_scales, b_words, b
             t = work.tile([P, 2048], BF16, name="grp", tag="grp", align_bytes=64)
             grp[k, h, c] = t
             if k == "W":
-                copy(E, t[:].rearrange("p (u s w j) -> p u s j w", u=4, s=32, w=4), w_raw[h, c][:].rearrange("p j (s u w) -> p u s j w", u=4, w=4))
+                copy(E, t[:].rearrange("p (u s w j) -> p u s j w", u=4, s=32, w=4), (w_rawf[c][:, :, h * 512 : (h + 1) * 512] if c else w_raw[h, 0][:]).rearrange("p j (s u w) -> p u s j w", u=4, w=4))
             else:
                 copy(E, t[:].rearrange("p (a w j) -> p a j w", w=4, j=4), x_raw[h, c][:].rearrange("p j (a w) -> p a j w", w=4))
 
@@ -165,32 +166,31 @@ def tile_concord_precision_gradient_s12_kernel(tc, a_words, a_scales, b_words, b
             co, sc = (w_codes, w_sc) if k == "W" else (x_codes, x_sc)
             nc.vector.quantize_mx(out=co[h, c][:].bitcast(FP8X4), scales=sc[h, c][:], in_=grp[k, h, c][:])
 
-        def K(h, l, u, c):
+        def K(h, l, p, f, c):
             if c == 0:
-                ps["K", h, l, u] = bank()
-            nc.tensor.matmul_mx(
-                out=ps["K", h, l, u][:],
-                lhsT=w_codes[h, c][:, u * 128 : (u + 1) * 128].bitcast(FP8X4),
-                lhsT_scale=w_sc[h, c][:, u * 128 : (u + 1) * 128],
-                rhs=x_codes[l, c][:].bitcast(FP8X4),
-                rhs_scale=x_sc[l, c][:],
-                start=(c == 0),
-                stop=(c == 3),
-            )
+                ps["K", h, l, p, f] = bank()
+            t = ps["K", h, l, p, f]
+            for e in range(2):
+                u = 2 * p + e
+                nc.tensor.matmul_mx(
+                    out=t[:, e * 256 : (e + 1) * 256],
+                    lhsT=w_codes[h, c][:, u * 128 : (u + 1) * 128].bitcast(FP8X4),
+                    lhsT_scale=w_sc[h, c][:, u * 128 : (u + 1) * 128],
+                    rhs=x_codes[l, c][:, f * 256 : (f + 1) * 256].bitcast(FP8X4),
+                    rhs_scale=x_sc[l, c][:, f * 256 : (f + 1) * 256],
+                    start=(c == 0 and e == 0),
+                    stop=(c == 3 and e == 1),
+                )
 
-        def eK(h, l, u, E):
-            copy(E, kun[h, l][:, u, :], ps["K", h, l, u][:])
+        def eK(h, l, p, f, E):
+            copy(E, kg[h, l][:, f * 256 : (f + 1) * 256, 2 * p : 2 * p + 2], ps["K", h, l, p, f][:].rearrange("p (u n) -> p n u", u=2))
 
-        def iK(h, l, E):
-            t = work.tile([P, 2048], BF16, name="grp", tag="grp", align_bytes=64)
-            grp["K", h, l] = t
-            copy(E, t[:].rearrange("p (a w u) -> p a u w", w=4, u=4), kun[h, l][:].rearrange("p u (a w) -> p a u w", w=4))
-
-        def qK(h, l):
-            nc.vector.quantize_mx(out=c_codes[:, h, l * 512 : (l + 1) * 512].bitcast(FP8X4), scales=c_sc[:, h, l * 512 : (l + 1) * 512], in_=grp["K", h, l][:])
+        def qK(h, l, f):
+            lo = l * 512 + f * 256
+            nc.vector.quantize_mx(out=c_codes[:, h, lo : lo + 256].bitcast(FP8X4), scales=c_sc[:, h, lo : lo + 256], in_=kg[h, l][:, f * 256 : (f + 1) * 256, :].rearrange("p n t -> p (n t)"))
 
         def span(p, b):
-            return (512, 128 * (b - 3)) if p == 2 else (0, 512)
+            return (512, 128 * (b - 3)) if p == 2 else (0, 512) if p == 1 else (0, 128 * (b + 1))
 
         def G(p, b):
             t = bank()
@@ -224,18 +224,22 @@ def tile_concord_precision_gradient_s12_kernel(tc, a_words, a_scales, b_words, b
                 nc.vector.scalar_tensor_tensor(out=g[:], in0=identx[:, z : z + n], scalar=d_neg[:, b : b + 1], in1=t[:, 0:n], op0=ALU.mult, op1=ALU.add)
             nc.sync.dma_start(out=out[b * 128 : (b + 1) * 128, lo : lo + n], in_=g[:])
 
+        def tr_strips(p, a):
+            return range(4, 8) if p == 0 else range(a + 1, 8) if p == 1 else range(a + 1, 4)
+
         def Tr(p, a):
             t = bank()
             ps["T", p, a] = t
-            for m, b in enumerate(range(4, 8) if p == 0 else range(a + 1, 8)):
-                src = gs[1, b][:, a * 128 : (a + 1) * 128] if p == 0 else gs[2, b][:, a * 128 - 512 : a * 128 - 384]
+            for m, b in enumerate(tr_strips(p, a)):
+                src = gs[1, b][:, a * 128 : (a + 1) * 128] if p == 0 else gs[0, b][:, a * 128 : (a + 1) * 128] if p == 2 else gs[2, b][:, a * 128 - 512 : a * 128 - 384]
                 nc.tensor.transpose(t[:, m * 128 : (m + 1) * 128], src, ident)
 
         def eT(p, a, E):
             u = ut[p, a]
-            n = 512 if p == 0 else 128 * (7 - a)
+            n = 128 * len(tr_strips(p, a))
+            hi = 512 if p == 2 else 1024
             copy(E, u[:], ps["T", p, a][:, 0:n])
-            nc.sync.dma_start(out=out[a * 128 : (a + 1) * 128, 1024 - n : 1024], in_=u[:])
+            nc.sync.dma_start(out=out[a * 128 : (a + 1) * 128, hi - n : hi], in_=u[:])
 
         def dT():
             t = bank()
@@ -246,202 +250,208 @@ def tile_concord_precision_gradient_s12_kernel(tc, a_words, a_scales, b_words, b
             nc.vector.reciprocal(out=d_rec[:], in_=ps["d"][:, 0:8])
             nc.vector.tensor_scalar(out=d_neg[:], in0=d_rec[:], scalar1=-1.0, scalar2=None, op0=ALU.mult)
 
-        dT()
-        pS()
         pB(0)
-        dN()
-        Om(0, 4)
+        pS()
+        Om(0, 2)
+        i("X", 0, 0, "V")
         Om(0, 3)
-        eO(0, 4, "V")
+        eO(0, 2, "S")
+        q("X", 0, 0)
+        i("W", 0, 2, "V")
+        i("W", 1, 2, "S")
+        Om(0, 1)
         Om(0, 0)
         pB(1)
-        eO(0, 3, "S")
-        Om(1, 1)
-        eO(0, 0, "S")
-        i("X", 0, 0, "V")
-        Om(1, 7)
-        eO(1, 1, "S")
-        Om(1, 4)
-        i("W", 0, 1, "S")
-        eO(1, 7, "V")
-        Om(0, 7)
-        q("X", 0, 0)
-        Om(0, 2)
-        i("W", 1, 0, "V")
-        Om(0, 1)
-        Om(1, 6)
-        eO(0, 2, "S")
-        q("W", 0, 1)
-        Om(1, 3)
-        eO(1, 6, "S")
-        q("W", 1, 0)
-        Om(0, 5)
-        eO(1, 4, "S")
-        i("W", 0, 2, "V")
-        Om(1, 0)
-        i("X", 0, 1, "S")
-        K(1, 0, 0, 0)
-        Om(1, 5)
-        eO(0, 1, "V")
-        K(1, 0, 3, 0)
-        i("W", 1, 1, "V")
-        K(1, 0, 2, 0)
-        eO(0, 5, "S")
         q("W", 0, 2)
-        i("W", 0, 0, "S")
-        q("X", 0, 1)
-        q("W", 1, 1)
-        i("W", 1, 2, "V")
-        K(1, 0, 2, 1)
-        K(1, 0, 1, 0)
-        eO(0, 7, "S")
-        K(1, 0, 0, 1)
-        K(1, 0, 3, 1)
-        q("W", 0, 0)
-        K(1, 0, 1, 1)
-        i("X", 0, 2, "S")
-        Om(1, 2)
-        i("W", 0, 3, "V")
+        Om(1, 1)
+        eO(0, 3, "S")
+        Om(1, 3)
         q("W", 1, 2)
+        eO(1, 1, "S")
+        i("W", 0, 1, "V")
+        Om(1, 2)
+        i("W", 1, 1, "S")
+        Om(1, 5)
+        eO(1, 2, "V")
+        Om(0, 4)
+        q("W", 0, 1)
+        Om(1, 7)
+        i("W", 0, 0, "V")
+        eO(0, 4, "S")
+        Om(1, 6)
+        eO(0, 0, "S")
+        Om(1, 0)
+        q("W", 1, 1)
+        eO(0, 1, "S")
+        Om(1, 4)
+        i("W", 1, 0, "V")
         eO(1, 0, "S")
-        q("X", 0, 2)
-        eO(1, 5, "S")
-        K(0, 0, 1, 0)
-        i("W", 1, 3, "V")
-        K(1, 0, 2, 2)
-        eO(1, 3, "S")
-        K(0, 0, 1, 1)
-        K(1, 0, 3, 2)
-        eO(1, 2, "S")
-        K(0, 0, 0, 0)
-        i("X", 0, 3, "V")
-        K(0, 0, 3, 0)
-        i("X", 1, 1, "S")
-        K(0, 0, 3, 1)
-        K(0, 0, 2, 0)
-        K(1, 0, 1, 2)
-        K(1, 0, 0, 2)
-        q("W", 1, 3)
-        K(0, 0, 2, 1)
-        K(0, 0, 1, 2)
-        q("X", 0, 3)
-        K(0, 0, 0, 1)
-        K(0, 0, 0, 2)
-        q("W", 0, 3)
-        K(0, 0, 3, 2)
-        i("X", 1, 2, "S")
-        K(1, 0, 3, 3)
-        i("X", 1, 0, "V")
-        K(1, 0, 2, 3)
-        K(0, 0, 3, 3)
-        K(0, 0, 2, 2)
-        K(1, 0, 1, 3)
-        K(1, 0, 0, 3)
-        eK(1, 0, 3, "V")
-        K(0, 0, 1, 3)
-        K(0, 0, 0, 3)
-        q("X", 1, 0)
-        eK(1, 0, 2, "S")
-        K(0, 0, 2, 3)
+        Om(0, 7)
+        eO(1, 6, "S")
+        q("W", 0, 0)
         Om(0, 6)
-        q("X", 1, 1)
-        eK(1, 0, 1, "S")
-        K(1, 1, 3, 0)
-        eK(0, 0, 3, "S")
+        eO(1, 4, "S")
+        i("X", 0, 1, "V")
+        eO(1, 3, "S")
+        K(0, 0, 1, 0, 0)
+        K(0, 0, 1, 1, 0)
+        eO(0, 7, "S")
+        Om(0, 5)
+        q("W", 1, 0)
+        i("X", 0, 2, "S")
+        q("X", 0, 1)
+        K(1, 0, 1, 0, 0)
+        K(1, 0, 0, 0, 0)
         eO(0, 6, "V")
-        K(0, 1, 3, 0)
-        K(1, 1, 3, 1)
-        eK(0, 0, 2, "S")
+        K(0, 0, 1, 1, 1)
+        i("X", 0, 3, "V")
+        K(0, 0, 0, 1, 0)
+        K(1, 0, 1, 0, 1)
+        eO(1, 7, "S")
+        K(1, 0, 0, 0, 1)
+        K(0, 0, 0, 1, 1)
+        eO(0, 5, "S")
+        q("X", 0, 2)
+        K(1, 0, 0, 1, 0)
+        K(1, 0, 0, 1, 1)
+        i("W", 1, 3, "S")
+        i("W", 0, 3, "V")
+        K(1, 0, 1, 0, 2)
+        K(0, 0, 1, 1, 2)
+        K(0, 0, 1, 0, 1)
+        K(1, 0, 1, 1, 0)
+        q("X", 0, 3)
+        K(1, 0, 0, 1, 2)
+        K(0, 0, 1, 0, 2)
+        K(0, 0, 0, 1, 2)
+        q("W", 0, 3)
+        K(1, 0, 1, 1, 1)
+        eO(1, 5, "S")
+        K(1, 0, 0, 0, 2)
+        q("W", 1, 3)
+        K(0, 0, 1, 1, 3)
+        i("X", 1, 1, "S")
+        K(1, 0, 1, 1, 2)
+        i("X", 1, 0, "V")
+        K(1, 0, 1, 1, 3)
+        K(1, 0, 0, 0, 3)
+        K(0, 0, 0, 0, 0)
+        K(1, 0, 0, 1, 3)
+        eK(1, 0, 1, 1, "V")
+        K(0, 0, 0, 0, 1)
+        K(1, 0, 1, 0, 3)
+        K(0, 0, 0, 0, 2)
+        q("X", 1, 0)
+        K(0, 0, 0, 0, 3)
+        eK(1, 0, 1, 0, "S")
+        K(0, 0, 0, 1, 3)
+        q("X", 1, 1)
+        K(1, 1, 1, 0, 0)
+        eK(1, 0, 0, 1, "S")
+        K(1, 1, 1, 1, 0)
+        i("X", 1, 2, "V")
+        K(1, 1, 1, 1, 1)
+        K(0, 0, 1, 0, 3)
+        eK(1, 0, 0, 0, "S")
+        K(1, 1, 1, 0, 1)
+        K(1, 1, 0, 0, 0)
+        K(1, 1, 0, 0, 1)
+        eK(0, 0, 1, 0, "S")
         q("X", 1, 2)
-        K(0, 1, 3, 1)
-        K(1, 1, 1, 0)
-        eK(1, 0, 0, "S")
-        qO(1, 1)
-        K(0, 1, 0, 0)
-        K(0, 1, 1, 0)
-        eK(0, 0, 0, "S")
+        K(0, 1, 1, 0, 0)
+        K(0, 1, 1, 0, 1)
         i("X", 1, 3, "V")
-        K(0, 1, 1, 1)
-        K(1, 1, 2, 0)
-        eK(0, 0, 1, "S")
-        K(1, 1, 1, 1)
-        K(0, 1, 2, 0)
-        iK(0, 0, "S")
-        K(0, 1, 3, 2)
-        K(1, 1, 0, 0)
-        q("X", 1, 3)
-        K(0, 1, 2, 1)
-        K(0, 1, 2, 2)
+        eK(0, 0, 0, 0, "S")
+        K(1, 1, 1, 0, 2)
+        K(0, 1, 1, 0, 2)
+        K(0, 1, 1, 1, 0)
+        eK(0, 0, 0, 1, "S")
+        K(0, 1, 1, 1, 1)
         qO(0, 0)
-        K(0, 1, 1, 2)
-        K(1, 1, 3, 2)
-        iK(1, 0, "V")
-        K(0, 1, 0, 1)
-        K(0, 1, 3, 3)
-        K(1, 1, 2, 1)
-        eK(0, 1, 3, "S")
-        K(1, 1, 2, 2)
-        K(1, 1, 3, 3)
-        qO(1, 0)
-        K(0, 1, 1, 3)
-        eK(1, 1, 3, "S")
-        K(1, 1, 2, 3)
-        qK(1, 0)
-        K(1, 1, 0, 1)
-        eK(1, 1, 2, "S")
-        K(1, 1, 0, 2)
-        qK(0, 0)
-        K(0, 1, 0, 2)
-        eK(0, 1, 1, "S")
-        K(0, 1, 0, 3)
-        K(0, 1, 2, 3)
-        eK(0, 1, 0, "V")
-        K(1, 1, 0, 3)
-        eK(0, 1, 2, "S")
-        K(1, 1, 1, 2)
+        K(0, 1, 0, 0, 0)
+        K(0, 1, 1, 1, 2)
+        eK(0, 0, 1, 1, "S")
+        K(0, 1, 0, 0, 1)
+        q("X", 1, 3)
+        K(0, 1, 0, 1, 0)
+        K(0, 1, 0, 0, 2)
+        qK(0, 0, 0)
+        K(0, 1, 0, 1, 1)
+        qK(1, 0, 0)
+        K(0, 1, 1, 0, 3)
+        qK(1, 0, 1)
+        K(0, 1, 0, 0, 3)
+        eK(0, 1, 1, 0, "S")
         qO(0, 1)
-        K(1, 1, 1, 3)
-        G(0, 0)
-        eK(1, 1, 1, "S")
-        eK(1, 1, 0, "V")
-        iK(0, 1, "S")
-        iK(1, 1, "V")
-        G(0, 1)
+        dT()
+        K(1, 1, 1, 0, 3)
+        K(1, 1, 0, 0, 2)
+        eK(0, 1, 0, 0, "V")
+        K(0, 1, 0, 1, 2)
+        eK(1, 1, 1, 0, "S")
+        K(1, 1, 0, 1, 0)
+        K(0, 1, 1, 1, 3)
+        qK(0, 0, 1)
+        K(1, 1, 0, 0, 3)
+        eK(0, 1, 1, 1, "S")
+        qO(1, 0)
+        K(1, 1, 1, 1, 2)
+        K(1, 1, 1, 1, 3)
+        qK(0, 1, 0)
+        K(0, 1, 0, 1, 3)
+        eK(1, 1, 0, 0, "S")
+        K(1, 1, 0, 1, 1)
+        dN()
+        qO(1, 1)
+        K(1, 1, 0, 1, 2)
         G(0, 2)
-        qK(1, 1)
-        qK(0, 1)
-        G(0, 3)
-        G(1, 4)
-        eG(0, 3, "V")
-        eG(0, 1, "V")
-        G(1, 7)
-        eG(1, 4, "V")
-        eG(0, 0, "V")
-        G(1, 5)
-        eG(1, 7, "S")
+        eK(0, 1, 0, 1, "S")
+        qK(1, 1, 0)
+        G(2, 5)
+        eK(1, 1, 1, 1, "S")
         eG(0, 2, "V")
-        G(1, 6)
+        K(1, 1, 0, 1, 3)
+        G(1, 5)
+        eK(1, 1, 0, 1, "S")
+        G(1, 4)
+        qK(1, 1, 1)
+        qK(0, 1, 1)
         eG(1, 5, "V")
+        G(1, 7)
+        eG(1, 4, "S")
+        eG(2, 5, "V")
+        G(1, 6)
+        eG(1, 7, "V")
         G(2, 7)
-        eG(1, 6, "S")
-        Tr(0, 0)
-        eG(2, 7, "V")
+        eG(1, 6, "V")
         Tr(0, 3)
-        eT(0, 0, "S")
-        Tr(0, 2)
+        eG(2, 7, "V")
+        Tr(0, 1)
         eT(0, 3, "V")
         G(2, 6)
-        eT(0, 2, "S")
-        Tr(0, 1)
-        eG(2, 6, "V")
-        G(2, 5)
         eT(0, 1, "S")
-        Tr(1, 5)
-        eG(2, 5, "V")
+        Tr(0, 2)
+        eG(2, 6, "V")
+        Tr(0, 0)
+        eT(0, 2, "S")
+        G(0, 3)
+        eT(0, 0, "V")
         Tr(1, 6)
+        eG(0, 3, "V")
+        Tr(1, 5)
+        eT(1, 6, "S")
+        G(0, 1)
         eT(1, 5, "V")
-        G(2, 4)
+        Tr(2, 1)
+        eG(0, 1, "V")
         Tr(1, 4)
+        eT(2, 1, "S")
+        Tr(2, 2)
+        eT(1, 4, "V")
+        Tr(2, 0)
+        eT(2, 2, "S")
+        G(2, 4)
+        eT(2, 0, "V")
+        G(0, 0)
         eG(2, 4, "V")
-        eT(1, 6, "V")
-        eT(1, 4, "S")
+        eG(0, 0, "V")

from contextlib import ExitStack

import concourse.mybir as mybir
from concourse.masks import make_identity

FLOPS = 2 * 1024 * 1024 * (1024 + 2048 + 1024)

F32 = mybir.dt.float32
BF16 = mybir.dt.bfloat16
I32 = mybir.dt.int32
U32 = mybir.dt.uint32
U8 = mybir.dt.uint8
FP8X4 = mybir.dt.float8_e4m3fn_x4
FP4X4 = mybir.dt.float4_e2m1fn_x4
ALU = mybir.AluOpType

P = 128


def tile_concord_precision_gradient_s12_kernel(tc, a_words, a_scales, b_words, b_scales, xw, x, d, out):
    nc = tc.nc
    with ExitStack() as ctx:
        keep = ctx.enter_context(tc.tile_pool(name="keep", bufs=1))
        work = ctx.enter_context(tc.tile_pool(name="work", bufs=5))
        psum = ctx.enter_context(tc.psum_pool(name="psum", bufs=8))
        ctx.enter_context(tc.manual_schedule())

        def kt(name, shape, dt):
            t = keep.tile(shape, dt, name=name, tag=name, align_bytes=64)
            return t

        def bank():
            t = psum.tile([P, 512], F32, name="bank", tag="bank")
            return t

        def copy(eng, dst, src):
            if eng == "S":
                nc.scalar.copy(out=dst, in_=src)
            else:
                nc.vector.tensor_copy(out=dst, in_=src)

        a_codes = [kt("a_codes%d" % h, [P, 2, 1024], U8) for h in range(2)]
        a_sc = kt("a_sc", [P, 2, 1024], U8)
        b_raw = [kt("b_raw%d" % h, [P, 2, 1024], U8) for h in range(2)]
        b_codes = [kt("b_codes%d" % h, [P, 2, 1024], U8) for h in range(2)]
        b_scr = kt("b_scr", [P, 2, 1024], U8)
        b_sc = kt("b_sc", [P, 2, 1024], U8)
        w_rawf = {c: kt("w_raw%d" % c, [P, 4, 1024], BF16) for c in range(1, 4)}
        w_raw = {(h, 0): kt("w_raw0%d" % h, [P, 4, 512], BF16) for h in range(2)}
        x_raw = {(h, c): kt("x_raw%d%d" % (h, c), [P, 4, 512], BF16) for c in range(4) for h in range(2)}
        w_codes = {(h, c): kt("w_codes%d%d" % (h, c), [P, 512], U32) for h in range(2) for c in range(4)}
        w_sc = {(h, c): kt("w_sc%d%d" % (h, c), [P, 512], U8) for h in range(2) for c in range(4)}
        x_codes = {(h, c): kt("x_codes%d%d" % (h, c), [P, 512], U32) for h in range(2) for c in range(4)}
        x_sc = {(h, c): kt("x_sc%d%d" % (h, c), [P, 512], U8) for h in range(2) for c in range(4)}
        o_codes = kt("o_codes", [P, 2, 1024], U32)
        o_sc = kt("o_sc", [P, 2, 1024], U8)
        c_codes = kt("c_codes", [P, 2, 1024], U32)
        c_sc = kt("c_sc", [P, 2, 1024], U8)
        og = {(h, q): kt("og%d%d" % (h, q), [P, 512, 4], BF16) for h in range(2) for q in range(2)}
        kg = {(h, l): kt("kg%d%d" % (h, l), [P, 512, 4], BF16) for h in range(2) for l in range(2)}
        gs = {(0, b): kt("gs0%d" % b, [P, 128 * (b + 1)], F32) for b in range(4)}
        for b in range(4, 8):
            gs[1, b] = kt("gs1%d" % b, [P, 512], F32)
            gs[2, b] = kt("gs2%d" % b, [P, 128 * (b - 3)], F32)
        ut = {(0, a): kt("ut0%d" % a, [P, 512], F32) for a in range(4)}
        for a in range(3):
            ut[2, a] = kt("ut2%d" % a, [P, 128 * (3 - a)], F32)
        for a in range(4, 7):
            ut[1, a] = kt("ut1%d" % a, [P, 128 * (7 - a)], F32)
        identx = kt("identx", [P, 512], F32)
        ident = identx[:, 384:512]
        d_row = kt("d_row", [P, 128], BF16)
        d_f32 = kt("d_f32", [P, 128], F32)
        d_rec = kt("d_rec", [P, 8], F32)
        d_neg = kt("d_neg", [P, 8], F32)
        grp = {}
        ps = {}

        nc.vector.memset(b_scr[:].bitcast(I32), 0)
        nc.vector.memset(a_sc[:].bitcast(I32), 0)

        def load_b(h):
            nc.sync.dma_start(out=b_raw[h][:].bitcast(I32), in_=b_words[:, :, h * 1024 : (h + 1) * 1024].bitcast(I32).rearrange("g p n -> p g n"))

        def load_a(q):
            nc.sync.dma_start(out=a_codes[q][:].bitcast(I32), in_=a_words[:, :, q * 1024 : (q + 1) * 1024].bitcast(I32).rearrange("g p n -> p g n"))

        def load_sc(eng, dst, src):
            for q in range(4):
                eng.dma_start(out=dst[32 * q : 32 * q + 4, :, :].bitcast(I32), in_=src[:, 4 * q : 4 * q + 4, :].bitcast(I32).rearrange("g q n -> q g n"))

        def load_w(c):
            nc.sync.dma_start(out=w_rawf[c][:], in_=xw[c * 512 : (c + 1) * 512, :].rearrange("(p j) w -> p j w", j=4))

        def load_k(dst, src, h, c):
            nc.sync.dma_start(out=dst[h, c][:], in_=src[c * 512 : (c + 1) * 512, h * 512 : (h + 1) * 512].rearrange("(p j) w -> p j w", j=4))

        load_a(0)
        load_sc(nc.sync, a_sc, a_scales)
        load_sc(nc.sync, b_scr, b_scales)
        load_b(0)
        load_k(x_raw, x, 0, 0)
        load_w(2)
        load_b(1)
        load_w(1)
        load_a(1)
        load_k(w_raw, xw, 0, 0)
        load_k(w_raw, xw, 1, 0)
        load_k(x_raw, x, 0, 1)
        load_k(x_raw, x, 0, 3)
        load_k(x_raw, x, 0, 2)
        load_w(3)
        load_k(x_raw, x, 1, 0)
        load_k(x_raw, x, 1, 2)
        load_k(x_raw, x, 1, 1)
        load_k(x_raw, x, 1, 3)
        nc.gpsimd.memset(d_row[:], 0.0)
        nc.gpsimd.dma_start(out=d_row[0:8, :], in_=d.rearrange("(a p) -> a p", p=128))
        nc.gpsimd.memset(identx[:], 0.0)
        make_identity(nc, ident)
        nc.gpsimd.tensor_copy(out=d_f32[:], in_=d_row[:])

        def pS():
            nc.vector.tensor_copy(
                out=b_sc[:].bitcast(I32).rearrange("p g (h u s) -> p g h u s", h=2, u=4),
                in_=b_scr[:].bitcast(I32).rearrange("p g (h s u) -> p g h u s", h=2, u=4),
            )

        def pB(h):
            nc.vector.tensor_copy(
                out=b_codes[h][:].bitcast(I32).rearrange("p g (u s w) -> p g u s w", u=4, w=2),
                in_=b_raw[h][:].bitcast(I32).rearrange("p g (s u w) -> p g u s w", u=4, w=2),
            )

        def Om(h, ib):
            t = bank()
            ps["O", h, ib] = t
            for u in range(4):
                for g in range(2):
                    nc.tensor.matmul_mx(
                        out=t[:, u * 128 : (u + 1) * 128],
                        lhsT=b_codes[h][:, g, u * 256 : (u + 1) * 256].bitcast(FP4X4),
                        lhsT_scale=b_sc[:, g, h * 512 + u * 128 : h * 512 + (u + 1) * 128],
                        rhs=a_codes[ib // 4][:, g, (ib % 4) * 256 : (ib % 4 + 1) * 256].bitcast(FP4X4),
                        rhs_scale=a_sc[:, g, ib * 128 : (ib + 1) * 128],
                        start=(g == 0),
                        stop=(g == 1),
                    )

        def eO(h, ib, E):
            n0 = (ib % 4) * 128
            copy(E, og[h, ib // 4][:, n0 : n0 + 128, :], ps["O", h, ib][:].rearrange("p (u n) -> p n u", u=4))

        def qO(h, q):
            nc.vector.quantize_mx(out=o_codes[:, h, q * 512 : (q + 1) * 512].bitcast(FP8X4), scales=o_sc[:, h, q * 512 : (q + 1) * 512], in_=og[h, q][:].rearrange("p n t -> p (n t)"))

        def i(k, h, c, E):
            t = work.tile([P, 2048], BF16, name="grp", tag="grp", align_bytes=64)
            grp[k, h, c] = t
            if k == "W":
                copy(E, t[:].rearrange("p (u s w j) -> p u s j w", u=4, s=32, w=4), (w_rawf[c][:, :, h * 512 : (h + 1) * 512] if c else w_raw[h, 0][:]).rearrange("p j (s u w) -> p u s j w", u=4, w=4))
            else:
                copy(E, t[:].rearrange("p (a w j) -> p a j w", w=4, j=4), x_raw[h, c][:].rearrange("p j (a w) -> p a j w", w=4))

        def q(k, h, c):
            co, sc = (w_codes, w_sc) if k == "W" else (x_codes, x_sc)
            nc.vector.quantize_mx(out=co[h, c][:].bitcast(FP8X4), scales=sc[h, c][:], in_=grp[k, h, c][:])

        def K(h, l, p, f, c):
            if c == 0:
                ps["K", h, l, p, f] = bank()
            t = ps["K", h, l, p, f]
            for e in range(2):
                u = 2 * p + e
                nc.tensor.matmul_mx(
                    out=t[:, e * 256 : (e + 1) * 256],
                    lhsT=w_codes[h, c][:, u * 128 : (u + 1) * 128].bitcast(FP8X4),
                    lhsT_scale=w_sc[h, c][:, u * 128 : (u + 1) * 128],
                    rhs=x_codes[l, c][:, f * 256 : (f + 1) * 256].bitcast(FP8X4),
                    rhs_scale=x_sc[l, c][:, f * 256 : (f + 1) * 256],
                    start=(c == 0 and e == 0),
                    stop=(c == 3 and e == 1),
                )

        def eK(h, l, p, f, E):
            copy(E, kg[h, l][:, f * 256 : (f + 1) * 256, 2 * p : 2 * p + 2], ps["K", h, l, p, f][:].rearrange("p (u n) -> p n u", u=2))

        def qK(h, l, f):
            lo = l * 512 + f * 256
            nc.vector.quantize_mx(out=c_codes[:, h, lo : lo + 256].bitcast(FP8X4), scales=c_sc[:, h, lo : lo + 256], in_=kg[h, l][:, f * 256 : (f + 1) * 256, :].rearrange("p n t -> p (n t)"))

        def span(p, b):
            return (512, 128 * (b - 3)) if p == 2 else (0, 512) if p == 1 else (0, 128 * (b + 1))

        def G(p, b):
            t = bank()
            ps["G", p, b] = t
            lo, n = span(p, b)
            bs = slice(b * 128, (b + 1) * 128)
            for o, w in ([(0, 256), (256, 128)] if n == 384 else [(0, n)]):
                ns = slice(lo + o, lo + o + w)
                step = 0
                for h in range(2):
                    for lc, ls, rc, rs in ((o_codes, o_sc, c_codes, c_sc), (c_codes, c_sc, o_codes, o_sc)):
                        nc.tensor.matmul_mx(
                            out=t[:, o : o + w],
                            lhsT=lc[:, h, bs].bitcast(FP8X4),
                            lhsT_scale=ls[:, h, bs],
                            rhs=rc[:, h, ns].bitcast(FP8X4),
                            rhs_scale=rs[:, h, ns],
                            start=(step == 0),
                            stop=(step == 3),
                        )
                        step += 1

        def eG(p, b, E):
            lo, n = span(p, b)
            t = ps["G", p, b]
            g = gs[p, b]
            if p == 1:
                copy(E, g[:], t[:])
            else:
                z = 384 - (b * 128 - lo)
                nc.vector.scalar_tensor_tensor(out=g[:], in0=identx[:, z : z + n], scalar=d_neg[:, b : b + 1], in1=t[:, 0:n], op0=ALU.mult, op1=ALU.add)
            nc.sync.dma_start(out=out[b * 128 : (b + 1) * 128, lo : lo + n], in_=g[:])

        def tr_strips(p, a):
            return range(4, 8) if p == 0 else range(a + 1, 8) if p == 1 else range(a + 1, 4)

        def Tr(p, a):
            t = bank()
            ps["T", p, a] = t
            for m, b in enumerate(tr_strips(p, a)):
                src = gs[1, b][:, a * 128 : (a + 1) * 128] if p == 0 else gs[0, b][:, a * 128 : (a + 1) * 128] if p == 2 else gs[2, b][:, a * 128 - 512 : a * 128 - 384]
                nc.tensor.transpose(t[:, m * 128 : (m + 1) * 128], src, ident)

        def eT(p, a, E):
            u = ut[p, a]
            n = 128 * len(tr_strips(p, a))
            hi = 512 if p == 2 else 1024
            copy(E, u[:], ps["T", p, a][:, 0:n])
            nc.sync.dma_start(out=out[a * 128 : (a + 1) * 128, hi - n : hi], in_=u[:])

        def dT():
            t = bank()
            ps["d"] = t
            nc.tensor.transpose(t[:, 0:128], d_f32[:], ident)

        def dN():
            nc.vector.reciprocal(out=d_rec[:], in_=ps["d"][:, 0:8])
            nc.vector.tensor_scalar(out=d_neg[:], in0=d_rec[:], scalar1=-1.0, scalar2=None, op0=ALU.mult)

        pB(0)
        pS()
        Om(0, 2)
        i("X", 0, 0, "V")
        Om(0, 3)
        eO(0, 2, "S")
        q("X", 0, 0)
        i("W", 0, 2, "V")
        i("W", 1, 2, "S")
        Om(0, 1)
        Om(0, 0)
        pB(1)
        q("W", 0, 2)
        Om(1, 1)
        eO(0, 3, "S")
        Om(1, 3)
        q("W", 1, 2)
        eO(1, 1, "S")
        i("W", 0, 1, "V")
        Om(1, 2)
        i("W", 1, 1, "S")
        Om(1, 5)
        eO(1, 2, "V")
        Om(0, 4)
        q("W", 0, 1)
        Om(1, 7)
        i("W", 0, 0, "V")
        eO(0, 4, "S")
        Om(1, 6)
        eO(0, 0, "S")
        Om(1, 0)
        q("W", 1, 1)
        eO(0, 1, "S")
        Om(1, 4)
        i("W", 1, 0, "V")
        eO(1, 0, "S")
        Om(0, 7)
        eO(1, 6, "S")
        q("W", 0, 0)
        Om(0, 6)
        eO(1, 4, "S")
        i("X", 0, 1, "V")
        eO(1, 3, "S")
        K(0, 0, 1, 0, 0)
        K(0, 0, 1, 1, 0)
        eO(0, 7, "S")
        Om(0, 5)
        q("W", 1, 0)
        i("X", 0, 2, "S")
        q("X", 0, 1)
        K(1, 0, 1, 0, 0)
        K(1, 0, 0, 0, 0)
        eO(0, 6, "V")
        K(0, 0, 1, 1, 1)
        i("X", 0, 3, "V")
        K(0, 0, 0, 1, 0)
        K(1, 0, 1, 0, 1)
        eO(1, 7, "S")
        K(1, 0, 0, 0, 1)
        K(0, 0, 0, 1, 1)
        eO(0, 5, "S")
        q("X", 0, 2)
        K(1, 0, 0, 1, 0)
        K(1, 0, 0, 1, 1)
        i("W", 1, 3, "S")
        i("W", 0, 3, "V")
        K(1, 0, 1, 0, 2)
        K(0, 0, 1, 1, 2)
        K(0, 0, 1, 0, 1)
        K(1, 0, 1, 1, 0)
        q("X", 0, 3)
        K(1, 0, 0, 1, 2)
        K(0, 0, 1, 0, 2)
        K(0, 0, 0, 1, 2)
        q("W", 0, 3)
        K(1, 0, 1, 1, 1)
        eO(1, 5, "S")
        K(1, 0, 0, 0, 2)
        q("W", 1, 3)
        K(0, 0, 1, 1, 3)
        i("X", 1, 1, "S")
        K(1, 0, 1, 1, 2)
        i("X", 1, 0, "V")
        K(1, 0, 1, 1, 3)
        K(1, 0, 0, 0, 3)
        K(0, 0, 0, 0, 0)
        K(1, 0, 0, 1, 3)
        eK(1, 0, 1, 1, "V")
        K(0, 0, 0, 0, 1)
        K(1, 0, 1, 0, 3)
        K(0, 0, 0, 0, 2)
        q("X", 1, 0)
        K(0, 0, 0, 0, 3)
        eK(1, 0, 1, 0, "S")
        K(0, 0, 0, 1, 3)
        q("X", 1, 1)
        K(1, 1, 1, 0, 0)
        eK(1, 0, 0, 1, "S")
        K(1, 1, 1, 1, 0)
        i("X", 1, 2, "V")
        K(1, 1, 1, 1, 1)
        K(0, 0, 1, 0, 3)
        eK(1, 0, 0, 0, "S")
        K(1, 1, 1, 0, 1)
        K(1, 1, 0, 0, 0)
        K(1, 1, 0, 0, 1)
        eK(0, 0, 1, 0, "S")
        q("X", 1, 2)
        K(0, 1, 1, 0, 0)
        K(0, 1, 1, 0, 1)
        i("X", 1, 3, "V")
        eK(0, 0, 0, 0, "S")
        K(1, 1, 1, 0, 2)
        K(0, 1, 1, 0, 2)
        K(0, 1, 1, 1, 0)
        eK(0, 0, 0, 1, "S")
        K(0, 1, 1, 1, 1)
        qO(0, 0)
        K(0, 1, 0, 0, 0)
        K(0, 1, 1, 1, 2)
        eK(0, 0, 1, 1, "S")
        K(0, 1, 0, 0, 1)
        q("X", 1, 3)
        K(0, 1, 0, 1, 0)
        K(0, 1, 0, 0, 2)
        qK(0, 0, 0)
        K(0, 1, 0, 1, 1)
        qK(1, 0, 0)
        K(0, 1, 1, 0, 3)
        qK(1, 0, 1)
        K(0, 1, 0, 0, 3)
        eK(0, 1, 1, 0, "S")
        qO(0, 1)
        dT()
        K(1, 1, 1, 0, 3)
        K(1, 1, 0, 0, 2)
        eK(0, 1, 0, 0, "V")
        K(0, 1, 0, 1, 2)
        eK(1, 1, 1, 0, "S")
        K(1, 1, 0, 1, 0)
        K(0, 1, 1, 1, 3)
        qK(0, 0, 1)
        K(1, 1, 0, 0, 3)
        eK(0, 1, 1, 1, "S")
        qO(1, 0)
        K(1, 1, 1, 1, 2)
        K(1, 1, 1, 1, 3)
        qK(0, 1, 0)
        K(0, 1, 0, 1, 3)
        eK(1, 1, 0, 0, "S")
        K(1, 1, 0, 1, 1)
        dN()
        qO(1, 1)
        K(1, 1, 0, 1, 2)
        G(0, 2)
        eK(0, 1, 0, 1, "S")
        qK(1, 1, 0)
        G(2, 5)
        eK(1, 1, 1, 1, "S")
        eG(0, 2, "V")
        K(1, 1, 0, 1, 3)
        G(1, 5)
        eK(1, 1, 0, 1, "S")
        G(1, 4)
        qK(1, 1, 1)
        qK(0, 1, 1)
        eG(1, 5, "V")
        G(1, 7)
        eG(1, 4, "S")
        eG(2, 5, "V")
        G(1, 6)
        eG(1, 7, "V")
        G(2, 7)
        eG(1, 6, "V")
        Tr(0, 3)
        eG(2, 7, "V")
        Tr(0, 1)
        eT(0, 3, "V")
        G(2, 6)
        eT(0, 1, "S")
        Tr(0, 2)
        eG(2, 6, "V")
        Tr(0, 0)
        eT(0, 2, "S")
        G(0, 3)
        eT(0, 0, "V")
        Tr(1, 6)
        eG(0, 3, "V")
        Tr(1, 5)
        eT(1, 6, "S")
        G(0, 1)
        eT(1, 5, "V")
        Tr(2, 1)
        eG(0, 1, "V")
        Tr(1, 4)
        eT(2, 1, "S")
        Tr(2, 2)
        eT(1, 4, "V")
        Tr(2, 0)
        eT(2, 2, "S")
        G(2, 4)
        eT(2, 0, "V")
        G(0, 0)
        eG(2, 4, "V")
        eG(0, 0, "V")
